import numpy as np, ml_dtypes
CORES = [2,42,66,74,82,90,114]
N = 7
import mx_ref
NC = 256
BF = ml_dtypes.bfloat16
def setup_inputs(rng):
    def f(*shape):
        return mx_ref.flush((rng.standard_normal(shape, dtype=np.float32) * np.exp2(rng.integers(-2, 3, shape[:-1] + (1,)))).astype(BF))
    return {"x": f(N, 128, 512), "w": f(N, 128, 4 * NC)}
def setup_inputs_blocks(rng):
    d = setup_inputs(rng)
    for k in ("x", "w"): d[k] = mx_ref.spread(d[k], rng, 4)
    return d
def setup_inputs_wide(rng):
    d = setup_inputs(rng)
    for k in ("x", "w"): d[k] = mx_ref.flush((d[k].astype(np.float32) * np.exp2(rng.integers(-6, 7, (N, 1, 1))).astype(np.float32)).astype(BF))
    return d
def setup_inputs_near(rng):
    d = setup_inputs(rng); v = d["w"].astype(np.float32).reshape(N, 128, -1, 4)
    d["w"] = mx_ref.flush((v[:1, :, :1] + v / 64).reshape(d["w"].shape).astype(BF))
    return d
def setup_inputs_twins(rng):
    d = setup_inputs(rng); v = d["w"].reshape(N, 128, -1, 4).copy(); a, b = rng.permutation(N)[:2]; i, j, k = rng.integers(0, v.shape[2], 3)
    v[a, :, i] = (v[a, :, i].astype(np.float32) * 8).astype(BF); v[a, :, j] = v[a, :, i]; v[b, :, k] = v[a, :, i]
    d["w"] = v.reshape(d["w"].shape)
    return d
def reference(x, w):
    W = [mx_ref.quantize(w[r]) for r in range(N)]
    y = np.zeros((N, 128, 2), np.float32)
    for j in range(N):
        X = mx_ref.quantize(x[j])
        L = np.concatenate([mx_ref.matmul(X, W[r]) for r in range(N)], axis=1)
        y[j][:, 0] = L.max(axis=1); y[j][:, 1] = L.argmax(axis=1)
    return {"y": y}

@@ -1,0 +1,124 @@
+from concourse.bass import DstId, RemoteDMATransfer
+from concourse.mybir import dt, AluOpType, AxisListType, ActivationFunctionType
+
+N = 7
+NC = 256
+LOW = -9.0e29
+BIG = 65536.0
+SLOT = 4
+
+SCRATCH = {
+    "xb": ("sbuf", [128, 512], "bfloat16"),
+    "wb": ("sbuf", [128, 4 * NC], "bfloat16"),
+    "wc": ("sbuf", [128, NC], "float8_e4m3fn_x4"),
+    "ws": ("sbuf", [128, NC], "uint8"),
+    "low": ("sbuf", [128, NC], "float32"),
+    "off": ("sbuf", [128, N], "float32"),
+    "pairs": ("sbuf", [128, SLOT * N], "float32"),
+    "key": ("sbuf", [128, N], "float32"),
+    "gidx": ("sbuf", [128, N], "float32"),
+    "res": ("sbuf", [128, 2 * N], "float32"),
+    "acc": ("psum", [128, 512 * N], "float32"),
+}
+SEMAPHORES = ["ldx", "ldw", "low", "off", "qx", "qw", "sent", "back", "own", "m1", "m2", "m3", "m4", "stored"]
+for _j in range(N):
+    SCRATCH["xc%d" % _j] = ("sbuf", [128, 128], "float8_e4m3fn_x4")
+    SCRATCH["xs%d" % _j] = ("sbuf", [128, 128], "uint8")
+    SCRATCH["run%d" % _j] = ("sbuf", [128, NC + 1], "float32")
+    SCRATCH["sgn%d" % _j] = ("sbuf", [128, NC], "bfloat16")
+    SEMAPHORES += ["arr%d" % _j, "mm%d" % _j, "sc%d" % _j, "ac%d" % _j]
+
+
+def slot(r):
+    return SLOT * (N - 1 - r)
+
+
+def bits(m):
+    return bin(m).count("1")
+
+
+def rank_program(g, core, T, topo):
+    rank = T.rank_of(core)
+    if rank is None:
+        return
+    A = AluOpType
+
+    def dst(c):
+        rid, pid, _ = topo.addr(c)
+        return DstId(rid=rid, pnc=pid)
+
+    dests = [(rank + k) % N for k in range(1, N)]
+    order = [(rank - k) % N for k in range(N)]
+    mask = {r: topo.mask(core, T.cores[r]) for r in dests}
+    xmask = mask[dests[0]]
+    for r in dests:
+        xmask &= mask[r]
+
+    g.sync.dma_start(T.xb[:], T.x[:]).then_inc(T.sem.ldx, 16)
+    g.sync.dma_start(T.wb[:], T.w[:]).then_inc(T.sem.ldw, 16)
+
+    g.iota(T.off[:], [[-NC, N]], NC * (N - 1), 0, allow_small_or_imprecise_dtypes=True).then_inc(T.sem.off, 1)
+    sent = 0
+    g.wait_ge(T.sem.qx, 1)
+    xc, xs = T["xc%d" % rank], T["xs%d" % rank]
+    arr = T.sem["arr%d" % rank]
+    for view in (xs[:], xc[:].bitcast(dt.uint8)):
+        g.remote_dma_fused([RemoteDMATransfer(dst_ids=[dst(T.cores[r]) for r in dests], dma_engine_mask=xmask,
+                                              remote_sem=arr, srcs=[view], dsts=[view for _ in dests])],
+                           local_sem=T.sem.sent)
+        sent += bits(xmask)
+    for j in order[1:]:
+        c = T.cores[j]
+        rid, pid, _ = topo.addr(c)
+        g.wait_ge(T.sem["ac%d" % j], 1)
+        g.remote_dma(T.pairs[:, slot(rank):slot(rank) + 2], T["run%d" % j][:, NC - 1:NC + 1],
+                     T.sem.back, T.sem.sent, pid, rid, mask[j])
+        sent += bits(mask[j])
+    g.wait_ge(T.sem.sent, sent)
+
+    g.vector.memset(T.low[:], LOW).then_inc(T.sem.low, 1)
+    g.vector.wait_ge(T.sem.ldx, 16)
+    g.vector.quantize_mx(xc[:], xs[:], T.xb[:]).then_inc(T.sem.qx, 1)
+    g.vector.wait_ge(T.sem.ldw, 16)
+    g.vector.quantize_mx(T.wc[:], T.ws[:], T.wb[:]).then_inc(T.sem.qw, 1)
+    g.vector.wait_ge(T.sem.low, 1)
+    for k, j in enumerate(order):
+        g.vector.wait_ge(T.sem["mm%d" % j], 1)
+        g.vector.tensor_tensor_scan(T["run%d" % j][:, 0:NC], T.acc[:, 512 * k:512 * k + NC], T.low[:], LOW,
+                                    A.max, A.max).then_inc(T.sem["sc%d" % j], 1)
+        if k == 1:
+            g.vector.wait_ge(T.sem["ac%d" % rank], 1)
+            g.vector.tensor_copy(T.pairs[:, slot(rank):slot(rank) + 2],
+                                 T["run%d" % rank][:, NC - 1:NC + 1]).then_inc(T.sem.own, 1)
+
+    g.tensor.wait_ge(T.sem.qw, 1)
+    for k, j in enumerate(order):
+        if k == 0:
+            g.tensor.wait_ge(T.sem.qx, 1)
+        else:
+            n = 2 * bits(topo.mask(T.cores[j], core))
+            g.tensor.wait_ge(T.sem["arr%d" % j], n)
+        g.tensor.matmul_mx(T.acc[:, 512 * k:512 * k + NC], T["xc%d" % j][:], T["xs%d" % j][:], T.wc[:], T.ws[:],
+                           True, True).then_inc(T.sem["mm%d" % j], 1)
+
+    for k, j in enumerate(order):
+        run = T["run%d" % j]
+        g.scalar.wait_ge(T.sem["sc%d" % j], 1)
+        g.scalar.activation(T["sgn%d" % j][:], run[:, 0:NC], ActivationFunctionType.Sign, bias=run[:, NC - 1:NC],
+                            scale=-1.0, accum_out=run[:, NC:NC + 1]).then_inc(T.sem["ac%d" % j], 1)
+
+    last = SLOT * (N - 1)
+    g.vector.wait_ge(T.sem.off, 1)
+    g.vector.wait_ge(T.sem.own, 1)
+    g.vector.wait_ge(T.sem.back, sum(bits(topo.mask(T.cores[r], core)) for r in dests))
+    g.vector.tensor_reduce(T.res[:, 2 * N - 2:2 * N - 1], T.pairs[:, 0:last + 1:SLOT], AxisListType.X, A.max).then_inc(T.sem.m1, 1)
+    g.vector.tensor_tensor(T.gidx[:], T.pairs[:, 1:last + 2:SLOT], T.off[:], A.add).then_inc(T.sem.m2, 1)
+    g.vector.wait_ge(T.sem.m1, 1)
+    g.vector.tensor_scalar(T.key[:], T.pairs[:, 0:last + 1:SLOT], T.res[:, 2 * N - 2:2 * N - 1], BIG, A.is_lt, A.mult).then_inc(T.sem.m3, 1)
+    g.vector.wait_ge(T.sem.m2, 1)
+    g.vector.wait_ge(T.sem.m3, 1)
+    g.vector.tensor_tensor_scan(T.res[:, 1:2 * N:2], T.key[:], T.gidx[:], 0.0, A.min, A.max).then_inc(T.sem.m4, 1)
+
+    g.sync.wait_ge(T.sem.m4, 1)
+    g.sync.dma_start(T.y[:], T.res[:, 2 * N - 2:2 * N]).then_inc(T.sem.stored, 16)
+    g.sync.wait_ge(T.sem.stored, 16)

@@ -7,11 +7,16 @@ LOW = -9.0e29
 BIG = 65536.0
 SLOT = 4
 
+RING = (0, 2, 6, 3, 5, 1, 4)
+XSTEPS = ((4, 2), (2, 2), (5, 1))
+
 SCRATCH = {
     "xb": ("sbuf", [128, 512], "bfloat16"),
     "wb": ("sbuf", [128, 4 * NC], "bfloat16"),
     "wc": ("sbuf", [128, NC], "float8_e4m3fn_x4"),
     "ws": ("sbuf", [128, NC], "uint8"),
+    "vc": ("sbuf", [128, NC], "float8_e4m3fn_x4"),
+    "vs": ("sbuf", [128, NC], "uint8"),
     "low": ("sbuf", [128, NC], "float32"),
     "off": ("sbuf", [128, N], "float32"),
     "pairs": ("sbuf", [128, SLOT * N], "float32"),
@@ -20,13 +25,13 @@ SCRATCH = {
     "res": ("sbuf", [128, 2 * N], "float32"),
     "acc": ("psum", [128, 512 * N], "float32"),
 }
-SEMAPHORES = ["ldx", "ldw", "low", "off", "qx", "qw", "sent", "back", "own", "m1", "m2", "m3", "m4", "stored"]
+SEMAPHORES = ["ldx", "ldw", "low", "off", "qx", "qw", "sent", "back", "warr", "m1", "m2", "m3", "m4", "stored"]
 for _j in range(N):
     SCRATCH["xc%d" % _j] = ("sbuf", [128, 128], "float8_e4m3fn_x4")
     SCRATCH["xs%d" % _j] = ("sbuf", [128, 128], "uint8")
     SCRATCH["run%d" % _j] = ("sbuf", [128, NC + 1], "float32")
     SCRATCH["sgn%d" % _j] = ("sbuf", [128, NC], "bfloat16")
-    SEMAPHORES += ["arr%d" % _j, "mm%d" % _j, "sc%d" % _j, "ac%d" % _j]
+    SEMAPHORES += ["arr%d" % _j, "mm%d" % _j, "sc%d" % _j, "ac%d" % _j, "own%d" % _j]
 
 
 def slot(r):
@@ -35,6 +40,12 @@ def slot(r):
 
 def bits(m):
     return bin(m).count("1")
+
+
+def shares(mask, n):
+    e = [i for i in range(mask.bit_length()) if mask >> i & 1]
+    k = len(e) // n
+    return [sum(1 << i for i in e[k * q:k * q + k]) for q in range(n)]
 
 
 def rank_program(g, core, T, topo):
@@ -47,9 +58,18 @@ def rank_program(g, core, T, topo):
         rid, pid, _ = topo.addr(c)
         return DstId(rid=rid, pnc=pid)
 
-    dests = [(rank + k) % N for k in range(1, N)]
-    order = [(rank - k) % N for k in range(N)]
-    mask = {r: topo.mask(core, T.cores[r]) for r in dests}
+    place = RING.index(rank)
+
+    def at(k):
+        return RING[(place + k) % N]
+
+    wdst, wsrc = at(1), at(-1)
+    dests = [at(k) for k, _ in XSTEPS]
+    held = (rank, wsrc)
+    products = [(rank, w) for w in held]
+    for k, n in XSTEPS:
+        products += [(at(-k), w) for w in held[:n]]
+    mask = {r: topo.mask(core, T.cores[r]) for r in range(N) if r != rank}
     xmask = mask[dests[0]]
     for r in dests:
         xmask &= mask[r]
@@ -59,21 +79,35 @@ def rank_program(g, core, T, topo):
 
     g.iota(T.off[:], [[-NC, N]], NC * (N - 1), 0, allow_small_or_imprecise_dtypes=True).then_inc(T.sem.off, 1)
     sent = 0
-    g.wait_ge(T.sem.qx, 1)
     xc, xs = T["xc%d" % rank], T["xs%d" % rank]
-    arr = T.sem["arr%d" % rank]
-    for view in (xs[:], xc[:].bitcast(dt.uint8)):
+
+    def send_x(view):
         g.remote_dma_fused([RemoteDMATransfer(dst_ids=[dst(T.cores[r]) for r in dests], dma_engine_mask=xmask,
-                                              remote_sem=arr, srcs=[view], dsts=[view for _ in dests])],
+                                              remote_sem=T.sem["arr%d" % rank], srcs=[view], dsts=[view for _ in dests])],
                            local_sem=T.sem.sent)
-        sent += bits(xmask)
-    for j in order[1:]:
-        c = T.cores[j]
-        rid, pid, _ = topo.addr(c)
-        g.wait_ge(T.sem["ac%d" % j], 1)
-        g.remote_dma(T.pairs[:, slot(rank):slot(rank) + 2], T["run%d" % j][:, NC - 1:NC + 1],
-                     T.sem.back, T.sem.sent, pid, rid, mask[j])
-        sent += bits(mask[j])
+        return bits(xmask)
+
+    def send_w(out, view):
+        rid, pid, _ = topo.addr(T.cores[wdst])
+        g.remote_dma(out, view, T.sem.warr, T.sem.sent, pid, rid, mask[wdst])
+        return bits(mask[wdst])
+
+    g.wait_ge(T.sem.qx, 1)
+    sent += send_x(xs[:])
+    g.wait_ge(T.sem.qw, 1)
+    sent += send_w(T.vs[:], T.ws[:])
+    sent += send_w(T.vc[:].bitcast(dt.uint8), T.wc[:].bitcast(dt.uint8))
+    sent += send_x(xc[:].bitcast(dt.uint8))
+    for k, n in XSTEPS:
+        j = at(-k)
+        trs = []
+        for w, part in zip(held[:n], shares(mask[j], n)):
+            p = products.index((j, w))
+            g.wait_ge(T.sem["ac%d" % p], 1)
+            trs.append(RemoteDMATransfer(dst_ids=[dst(T.cores[j])], dma_engine_mask=part, remote_sem=T.sem.back,
+                                         srcs=[T["run%d" % p][:, NC - 1:NC + 1]], dsts=[T.pairs[:, slot(w):slot(w) + 2]]))
+            sent += bits(part)
+        g.remote_dma_fused(trs, local_sem=T.sem.sent)
     g.wait_ge(T.sem.sent, sent)
 
     g.vector.memset(T.low[:], LOW).then_inc(T.sem.low, 1)
@@ -82,35 +116,43 @@ def rank_program(g, core, T, topo):
     g.vector.wait_ge(T.sem.ldw, 16)
     g.vector.quantize_mx(T.wc[:], T.ws[:], T.wb[:]).then_inc(T.sem.qw, 1)
     g.vector.wait_ge(T.sem.low, 1)
-    for k, j in enumerate(order):
-        g.vector.wait_ge(T.sem["mm%d" % j], 1)
-        g.vector.tensor_tensor_scan(T["run%d" % j][:, 0:NC], T.acc[:, 512 * k:512 * k + NC], T.low[:], LOW,
-                                    A.max, A.max).then_inc(T.sem["sc%d" % j], 1)
-        if k == 1:
-            g.vector.wait_ge(T.sem["ac%d" % rank], 1)
-            g.vector.tensor_copy(T.pairs[:, slot(rank):slot(rank) + 2],
-                                 T["run%d" % rank][:, NC - 1:NC + 1]).then_inc(T.sem.own, 1)
+    for p, (j, w) in enumerate(products):
+        run = T["run%d" % p]
+        g.vector.wait_ge(T.sem["mm%d" % p], 1)
+        g.vector.tensor_tensor_scan(run[:, 0:NC], T.acc[:, 512 * p:512 * p + NC], T.low[:], LOW,
+                                    A.max, A.max).then_inc(T.sem["sc%d" % p], 1)
+        if j == rank:
+            g.vector.wait_ge(T.sem["sc%d" % p], 1)
+            g.vector.tensor_copy(T.pairs[:, slot(w):slot(w) + 1], run[:, NC - 1:NC]).then_inc(T.sem["own%d" % p], 1)
 
     g.tensor.wait_ge(T.sem.qw, 1)
-    for k, j in enumerate(order):
-        if k == 0:
-            g.tensor.wait_ge(T.sem.qx, 1)
-        else:
-            n = 2 * bits(topo.mask(T.cores[j], core))
-            g.tensor.wait_ge(T.sem["arr%d" % j], n)
-        g.tensor.matmul_mx(T.acc[:, 512 * k:512 * k + NC], T["xc%d" % j][:], T["xs%d" % j][:], T.wc[:], T.ws[:],
-                           True, True).then_inc(T.sem["mm%d" % j], 1)
+    g.tensor.wait_ge(T.sem.qx, 1)
+    for p, (j, w) in enumerate(products):
+        if j == rank and w != rank:
+            g.tensor.wait_ge(T.sem.warr, 2 * bits(topo.mask(T.cores[w], core)))
+        elif j != rank and w == rank:
+            g.tensor.wait_ge(T.sem["arr%d" % j], 2 * bits(topo.mask(T.cores[j], core)))
+        wq, wp = (T.wc, T.ws) if w == rank else (T.vc, T.vs)
+        g.tensor.matmul_mx(T.acc[:, 512 * p:512 * p + NC], T["xc%d" % j][:], T["xs%d" % j][:], wq[:], wp[:],
+                           True, True).then_inc(T.sem["mm%d" % p], 1)
 
-    for k, j in enumerate(order):
-        run = T["run%d" % j]
-        g.scalar.wait_ge(T.sem["sc%d" % j], 1)
-        g.scalar.activation(T["sgn%d" % j][:], run[:, 0:NC], ActivationFunctionType.Sign, bias=run[:, NC - 1:NC],
-                            scale=-1.0, accum_out=run[:, NC:NC + 1]).then_inc(T.sem["ac%d" % j], 1)
+    for p, (j, w) in enumerate(products):
+        run = T["run%d" % p]
+        out = T.pairs[:, slot(w) + 1:slot(w) + 2] if j == rank else run[:, NC:NC + 1]
+        g.scalar.wait_ge(T.sem["sc%d" % p], 1)
+        g.scalar.activation(T["sgn%d" % p][:], run[:, 0:NC], ActivationFunctionType.Sign, bias=run[:, NC - 1:NC],
+                            scale=-1.0, accum_out=out).then_inc(T.sem["ac%d" % p], 1)
 
     last = SLOT * (N - 1)
     g.vector.wait_ge(T.sem.off, 1)
-    g.vector.wait_ge(T.sem.own, 1)
-    g.vector.wait_ge(T.sem.back, sum(bits(topo.mask(T.cores[r], core)) for r in dests))
+    for p, (j, w) in enumerate(products):
+        if j == rank:
+            g.vector.wait_ge(T.sem["own%d" % p], 1)
+            g.vector.wait_ge(T.sem["ac%d" % p], 1)
+    back = 0
+    for k, n in XSTEPS:
+        back += sum(bits(m) for m in shares(topo.mask(T.cores[at(k)], core), n))
+    g.vector.wait_ge(T.sem.back, back)
     g.vector.tensor_reduce(T.res[:, 2 * N - 2:2 * N - 1], T.pairs[:, 0:last + 1:SLOT], AxisListType.X, A.max).then_inc(T.sem.m1, 1)
     g.vector.tensor_tensor(T.gidx[:], T.pairs[:, 1:last + 2:SLOT], T.off[:], A.add).then_inc(T.sem.m2, 1)
     g.vector.wait_ge(T.sem.m1, 1)

@@ -5,47 +5,42 @@ N = 7
 NC = 256
 LOW = -9.0e29
 BIG = 65536.0
-SLOT = 4
 
-RING = (0, 2, 6, 3, 5, 1, 4)
-XSTEPS = ((4, 2), (2, 2), (5, 1))
+RING = (0, 2, 1, 5, 3, 6, 4)
+XTO = (5, 3)
+WTO = (1, 6)
+HOME, VISIT = 3, 2
+LAND = 2 * HOME * NC
+FIRST = LAND - 2 * HOME
 
 SCRATCH = {
     "xb": ("sbuf", [128, 512], "bfloat16"),
     "wb": ("sbuf", [128, 4 * NC], "bfloat16"),
-    "wc": ("sbuf", [128, NC], "float8_e4m3fn_x4"),
-    "ws": ("sbuf", [128, NC], "uint8"),
-    "vc": ("sbuf", [128, NC], "float8_e4m3fn_x4"),
-    "vs": ("sbuf", [128, NC], "uint8"),
     "low": ("sbuf", [128, NC], "float32"),
     "off": ("sbuf", [128, N], "float32"),
-    "pairs": ("sbuf", [128, SLOT * N], "float32"),
-    "key": ("sbuf", [128, N], "float32"),
-    "gidx": ("sbuf", [128, N], "float32"),
-    "res": ("sbuf", [128, 2 * N], "float32"),
+    "step0": ("sbuf", [128, 2 * N], "float32"),
+    "step1": ("sbuf", [128, 2 * N], "float32"),
+    "res": ("sbuf", [128, 4 * N], "float32"),
+    "home": ("sbuf", [128, LAND + 2 * VISIT * len(XTO)], "float32"),
+    "visit1": ("sbuf", [128, 2 * VISIT * NC], "float32"),
+    "visit2": ("sbuf", [128, 2 * VISIT * NC], "float32"),
     "acc": ("psum", [128, 512 * N], "float32"),
 }
-SEMAPHORES = ["ldx", "ldw", "low", "off", "qx", "qw", "sent", "back", "warr", "m1", "m2", "m3", "m4", "stored"]
+SEMAPHORES = ["ldx", "ldw", "low", "off", "large", "qx", "qw", "warr1", "warr2", "sent", "back", "m1", "m2", "m3", "m4", "stored"]
+for _j in range(1 + len(WTO)):
+    SCRATCH["wc%d" % _j] = ("sbuf", [128, NC], "float8_e4m3fn_x4")
+    SCRATCH["ws%d" % _j] = ("sbuf", [128, NC], "uint8")
 for _j in range(N):
     SCRATCH["xc%d" % _j] = ("sbuf", [128, 128], "float8_e4m3fn_x4")
     SCRATCH["xs%d" % _j] = ("sbuf", [128, 128], "uint8")
-    SCRATCH["run%d" % _j] = ("sbuf", [128, NC + 1], "float32")
     SCRATCH["sgn%d" % _j] = ("sbuf", [128, NC], "bfloat16")
-    SEMAPHORES += ["arr%d" % _j, "mm%d" % _j, "sc%d" % _j, "ac%d" % _j, "own%d" % _j]
+    SEMAPHORES += ["arr%d" % _j, "mm%d" % _j, "sc%d" % _j, "ac%d" % _j]
 
-
-def slot(r):
-    return SLOT * (N - 1 - r)
+PRODUCTS = [(0, 0), (1, 0), (2, 0), (1, 1), (2, 1), (0, 1), (0, 2)]
 
 
 def bits(m):
     return bin(m).count("1")
-
-
-def shares(mask, n):
-    e = [i for i in range(mask.bit_length()) if mask >> i & 1]
-    k = len(e) // n
-    return [sum(1 << i for i in e[k * q:k * q + k]) for q in range(n)]
 
 
 def rank_program(g, core, T, topo):
@@ -53,114 +48,115 @@ def rank_program(g, core, T, topo):
     if rank is None:
         return
     A = AluOpType
-
-    def dst(c):
-        rid, pid, _ = topo.addr(c)
-        return DstId(rid=rid, pnc=pid)
-
     place = RING.index(rank)
 
     def at(k):
         return RING[(place + k) % N]
 
-    wdst, wsrc = at(1), at(-1)
-    dests = [at(k) for k, _ in XSTEPS]
-    held = (rank, wsrc)
-    products = [(rank, w) for w in held]
-    for k, n in XSTEPS:
-        products += [(at(-k), w) for w in held[:n]]
-    mask = {r: topo.mask(core, T.cores[r]) for r in range(N) if r != rank}
-    xmask = mask[dests[0]]
-    for r in dests:
-        xmask &= mask[r]
+    def dst(r):
+        rid, pid, _ = topo.addr(T.cores[r])
+        return DstId(rid=rid, pnc=pid)
+
+    def out_mask(r):
+        return topo.mask(core, T.cores[r])
+
+    def in_count(r):
+        return bits(topo.mask(T.cores[r], core))
+
+    def spot(x, w):
+        buf, n = (T.home, HOME) if x == 0 else (T["visit%d" % x], VISIT)
+        last = 2 * n * (NC - 1) + 2 * w
+        return buf, slice(2 * w, last + 1, 2 * n), last
+
+    xrank = [rank] + [at(-k) for k in XTO]
+    shards = [at(-k) for k in (0,) + WTO] + [at(k - v) for k in XTO for v in (0, WTO[0])]
 
     g.sync.dma_start(T.xb[:], T.x[:]).then_inc(T.sem.ldx, 16)
     g.sync.dma_start(T.wb[:], T.w[:]).then_inc(T.sem.ldw, 16)
 
-    g.iota(T.off[:], [[-NC, N]], NC * (N - 1), 0, allow_small_or_imprecise_dtypes=True).then_inc(T.sem.off, 1)
     sent = 0
     xc, xs = T["xc%d" % rank], T["xs%d" % rank]
-
-    def send_x(view):
-        g.remote_dma_fused([RemoteDMATransfer(dst_ids=[dst(T.cores[r]) for r in dests], dma_engine_mask=xmask,
+    dests = [at(k) for k in XTO]
+    xmask = out_mask(dests[0])
+    for r in dests:
+        xmask &= out_mask(r)
+    g.wait_ge(T.sem.qx, 1)
+    for view in (xs[:], xc[:].bitcast(dt.uint8)):
+        g.remote_dma_fused([RemoteDMATransfer(dst_ids=[dst(r) for r in dests], dma_engine_mask=xmask,
                                               remote_sem=T.sem["arr%d" % rank], srcs=[view], dsts=[view for _ in dests])],
                            local_sem=T.sem.sent)
-        return bits(xmask)
-
-    def send_w(out, view):
-        rid, pid, _ = topo.addr(T.cores[wdst])
-        g.remote_dma(out, view, T.sem.warr, T.sem.sent, pid, rid, mask[wdst])
-        return bits(mask[wdst])
-
-    g.wait_ge(T.sem.qx, 1)
-    sent += send_x(xs[:])
+        sent += bits(xmask)
     g.wait_ge(T.sem.qw, 1)
-    sent += send_w(T.vs[:], T.ws[:])
-    sent += send_w(T.vc[:].bitcast(dt.uint8), T.wc[:].bitcast(dt.uint8))
-    sent += send_x(xc[:].bitcast(dt.uint8))
-    for k, n in XSTEPS:
-        j = at(-k)
-        trs = []
-        for w, part in zip(held[:n], shares(mask[j], n)):
-            p = products.index((j, w))
-            g.wait_ge(T.sem["ac%d" % p], 1)
-            trs.append(RemoteDMATransfer(dst_ids=[dst(T.cores[j])], dma_engine_mask=part, remote_sem=T.sem.back,
-                                         srcs=[T["run%d" % p][:, NC - 1:NC + 1]], dsts=[T.pairs[:, slot(w):slot(w) + 2]]))
-            sent += bits(part)
-        g.remote_dma_fused(trs, local_sem=T.sem.sent)
+    for w, k in enumerate(WTO, 1):
+        r = at(k)
+        rid, pid, _ = topo.addr(T.cores[r])
+        for out, view in ((T["ws%d" % w][:], T.ws0[:]), (T["wc%d" % w][:].bitcast(dt.uint8), T.wc0[:].bitcast(dt.uint8))):
+            g.remote_dma(out, view, T.sem["warr%d" % w], T.sem.sent, pid, rid, out_mask(r))
+            sent += bits(out_mask(r))
+    for x in range(1, 1 + len(XTO)):
+        r = xrank[x]
+        rid, pid, _ = topo.addr(T.cores[r])
+        for p, (px, _) in enumerate(PRODUCTS):
+            if px == x:
+                g.wait_ge(T.sem["ac%d" % p], 1)
+        buf, _, first = spot(x, 0)
+        land = LAND + 2 * VISIT * (x - 1)
+        g.remote_dma(T.home[:, land:land + 2 * VISIT], buf[:, first:first + 2 * VISIT], T.sem.back, T.sem.sent, pid, rid, out_mask(r))
+        sent += bits(out_mask(r))
     g.wait_ge(T.sem.sent, sent)
 
     g.vector.memset(T.low[:], LOW).then_inc(T.sem.low, 1)
+    for i, r in enumerate(shards):
+        g.vector.memset(T.off[:, i:i + 1], float(NC * r)).then_inc(T.sem.off, 1)
+    g.vector.memset(T.step1[:], BIG).then_inc(T.sem.large, 1)
     g.vector.wait_ge(T.sem.ldx, 16)
     g.vector.quantize_mx(xc[:], xs[:], T.xb[:]).then_inc(T.sem.qx, 1)
     g.vector.wait_ge(T.sem.ldw, 16)
-    g.vector.quantize_mx(T.wc[:], T.ws[:], T.wb[:]).then_inc(T.sem.qw, 1)
+    g.vector.quantize_mx(T.wc0[:], T.ws0[:], T.wb[:]).then_inc(T.sem.qw, 1)
     g.vector.wait_ge(T.sem.low, 1)
-    for p, (j, w) in enumerate(products):
-        run = T["run%d" % p]
+    for p, (x, w) in enumerate(PRODUCTS):
+        buf, cols, _ = spot(x, w)
         g.vector.wait_ge(T.sem["mm%d" % p], 1)
-        g.vector.tensor_tensor_scan(run[:, 0:NC], T.acc[:, 512 * p:512 * p + NC], T.low[:], LOW,
+        g.vector.tensor_tensor_scan(buf[:, cols], T.acc[:, 512 * p:512 * p + NC], T.low[:], LOW,
                                     A.max, A.max).then_inc(T.sem["sc%d" % p], 1)
-        if j == rank:
-            g.vector.wait_ge(T.sem["sc%d" % p], 1)
-            g.vector.tensor_copy(T.pairs[:, slot(w):slot(w) + 1], run[:, NC - 1:NC]).then_inc(T.sem["own%d" % p], 1)
 
-    g.tensor.wait_ge(T.sem.qw, 1)
     g.tensor.wait_ge(T.sem.qx, 1)
-    for p, (j, w) in enumerate(products):
-        if j == rank and w != rank:
-            g.tensor.wait_ge(T.sem.warr, 2 * bits(topo.mask(T.cores[w], core)))
-        elif j != rank and w == rank:
-            g.tensor.wait_ge(T.sem["arr%d" % j], 2 * bits(topo.mask(T.cores[j], core)))
-        wq, wp = (T.wc, T.ws) if w == rank else (T.vc, T.vs)
-        g.tensor.matmul_mx(T.acc[:, 512 * p:512 * p + NC], T["xc%d" % j][:], T["xs%d" % j][:], wq[:], wp[:],
-                           True, True).then_inc(T.sem["mm%d" % p], 1)
+    g.tensor.wait_ge(T.sem.qw, 1)
+    seen = {("x", 0), ("w", 0)}
+    for p, (x, w) in enumerate(PRODUCTS):
+        if ("x", x) not in seen:
+            seen.add(("x", x))
+            g.tensor.wait_ge(T.sem["arr%d" % xrank[x]], 2 * in_count(xrank[x]))
+        if ("w", w) not in seen:
+            seen.add(("w", w))
+            g.tensor.wait_ge(T.sem["warr%d" % w], 2 * in_count(at(-WTO[w - 1])))
+        g.tensor.matmul_mx(T.acc[:, 512 * p:512 * p + NC], T["xc%d" % xrank[x]][:], T["xs%d" % xrank[x]][:],
+                           T["wc%d" % w][:], T["ws%d" % w][:], True, True).then_inc(T.sem["mm%d" % p], 1)
 
-    for p, (j, w) in enumerate(products):
-        run = T["run%d" % p]
-        out = T.pairs[:, slot(w) + 1:slot(w) + 2] if j == rank else run[:, NC:NC + 1]
+    for p, (x, w) in enumerate(PRODUCTS):
+        buf, cols, last = spot(x, w)
         g.scalar.wait_ge(T.sem["sc%d" % p], 1)
-        g.scalar.activation(T["sgn%d" % p][:], run[:, 0:NC], ActivationFunctionType.Sign, bias=run[:, NC - 1:NC],
-                            scale=-1.0, accum_out=out).then_inc(T.sem["ac%d" % p], 1)
+        g.scalar.activation(T["sgn%d" % p][:], buf[:, cols], ActivationFunctionType.Sign, bias=buf[:, last:last + 1],
+                            scale=-1.0, accum_out=buf[:, last + 1:last + 2]).then_inc(T.sem["ac%d" % p], 1)
 
-    last = SLOT * (N - 1)
-    g.vector.wait_ge(T.sem.off, 1)
-    for p, (j, w) in enumerate(products):
-        if j == rank:
-            g.vector.wait_ge(T.sem["own%d" % p], 1)
+    end = FIRST + 2 * N
+    maxima, indices = T.home[:, FIRST:end:2], T.home[:, FIRST + 1:end:2]
+    best = T.res[:, 4 * N - 2:4 * N - 1]
+    g.vector.wait_ge(T.sem.off, N)
+    g.vector.wait_ge(T.sem.large, 1)
+    for p, (x, w) in enumerate(PRODUCTS):
+        if x == 0:
             g.vector.wait_ge(T.sem["ac%d" % p], 1)
-    back = 0
-    for k, n in XSTEPS:
-        back += sum(bits(m) for m in shares(topo.mask(T.cores[at(k)], core), n))
-    g.vector.wait_ge(T.sem.back, back)
-    g.vector.tensor_reduce(T.res[:, 2 * N - 2:2 * N - 1], T.pairs[:, 0:last + 1:SLOT], AxisListType.X, A.max).then_inc(T.sem.m1, 1)
-    g.vector.tensor_tensor(T.gidx[:], T.pairs[:, 1:last + 2:SLOT], T.off[:], A.add).then_inc(T.sem.m2, 1)
+    g.vector.wait_ge(T.sem.back, sum(in_count(r) for r in dests))
+    g.vector.tensor_reduce(best, maxima, AxisListType.X, A.max).then_inc(T.sem.m1, 1)
+    g.vector.tensor_tensor(T.step1[:, 0:2 * N:2], indices, T.off[:], A.add).then_inc(T.sem.m2, 1)
     g.vector.wait_ge(T.sem.m1, 1)
-    g.vector.tensor_scalar(T.key[:], T.pairs[:, 0:last + 1:SLOT], T.res[:, 2 * N - 2:2 * N - 1], BIG, A.is_lt, A.mult).then_inc(T.sem.m3, 1)
+    g.vector.tensor_scalar(T.step0[:, 0:2 * N:2], maxima, best, -BIG, A.is_lt, A.mult).then_inc(T.sem.m3, 1)
+    g.vector.tensor_scalar(T.step0[:, 1:2 * N:2], maxima, best, BIG, A.is_lt, A.mult).then_inc(T.sem.m3, 1)
     g.vector.wait_ge(T.sem.m2, 1)
-    g.vector.wait_ge(T.sem.m3, 1)
-    g.vector.tensor_tensor_scan(T.res[:, 1:2 * N:2], T.key[:], T.gidx[:], 0.0, A.min, A.max).then_inc(T.sem.m4, 1)
+    g.vector.wait_ge(T.sem.m3, 2)
+    g.vector.tensor_tensor_scan(T.res[:, 1:4 * N:2], T.step0[:], T.step1[:], BIG, A.add, A.min).then_inc(T.sem.m4, 1)
 
     g.sync.wait_ge(T.sem.m4, 1)
-    g.sync.dma_start(T.y[:], T.res[:, 2 * N - 2:2 * N]).then_inc(T.sem.stored, 16)
+    g.sync.dma_start(T.y[:], T.res[:, 4 * N - 2:4 * N]).then_inc(T.sem.stored, 16)
     g.sync.wait_ge(T.sem.stored, 16)

@@ -2,41 +2,49 @@ from concourse.bass import DstId, RemoteDMATransfer
 from concourse.mybir import dt, AluOpType, AxisListType, ActivationFunctionType
 
 N = 7
+GRID = 128
 NC = 256
+NH = NC // 2
 LOW = -9.0e29
 BIG = 65536.0
 
 RING = (0, 2, 1, 5, 3, 6, 4)
 XTO = (5, 3)
-WTO = (1, 6)
-HOME, VISIT = 3, 2
-LAND = 2 * HOME * NC
-FIRST = LAND - 2 * HOME
+WTO = (1, 6, 5)
+
+ALL, HA, HB = (0, NC), (0, NH), (NH, NC)
+PRODUCTS = [(0, 0, ALL), (1, 0, ALL), (2, 0, ALL), (2, 1, HA), (1, 1, HA), (1, 1, HB), (0, 1, ALL), (0, 2, HB), (0, 2, HA), (0, 3, HB)]
+PAIRS = [[p for p in range(len(PRODUCTS)) if PRODUCTS[p][0] == x] for x in range(3)]
+NP = len(PRODUCTS)
+BANKS = 8
+LAND = 2 * len(PAIRS[0]) * NC
+FIRST = LAND - 2 * len(PAIRS[0])
+STEPS = 3 * NP
 
 SCRATCH = {
     "xb": ("sbuf", [128, 512], "bfloat16"),
     "wb": ("sbuf", [128, 4 * NC], "bfloat16"),
     "low": ("sbuf", [128, NC], "float32"),
-    "off": ("sbuf", [128, N], "float32"),
-    "step0": ("sbuf", [128, 2 * N], "float32"),
-    "step1": ("sbuf", [128, 2 * N], "float32"),
-    "res": ("sbuf", [128, 4 * N], "float32"),
-    "home": ("sbuf", [128, LAND + 2 * VISIT * len(XTO)], "float32"),
-    "visit1": ("sbuf", [128, 2 * VISIT * NC], "float32"),
-    "visit2": ("sbuf", [128, 2 * VISIT * NC], "float32"),
-    "acc": ("psum", [128, 512 * N], "float32"),
+    "step0": ("sbuf", [128, STEPS], "float32"),
+    "step1": ("sbuf", [128, STEPS], "float32"),
+    "res": ("sbuf", [128, 2 * STEPS], "float32"),
+    "visit0": ("sbuf", [128, LAND + 2 * (len(PAIRS[1]) + len(PAIRS[2]))], "float32"),
+    "visit1": ("sbuf", [128, 2 * len(PAIRS[1]) * NC], "float32"),
+    "visit2": ("sbuf", [128, 2 * len(PAIRS[2]) * NC], "float32"),
+    "acc": ("psum", [128, 512 * BANKS], "float32"),
 }
-SEMAPHORES = ["ldx", "ldw", "low", "off", "large", "qx", "qw", "warr1", "warr2", "sent", "back", "m1", "m2", "m3", "m4", "stored"]
-for _j in range(1 + len(WTO)):
+SEMAPHORES = ["ldx", "ldw", "low", "turn", "large", "qx", "qw", "w1a", "w1b", "w2a", "w2b", "w3b", "plane", "codes",
+              "sent", "back", "m1", "m2", "m3", "m4", "stored"]
+for _j in range(4):
     SCRATCH["wc%d" % _j] = ("sbuf", [128, NC], "float8_e4m3fn_x4")
     SCRATCH["ws%d" % _j] = ("sbuf", [128, NC], "uint8")
 for _j in range(N):
     SCRATCH["xc%d" % _j] = ("sbuf", [128, 128], "float8_e4m3fn_x4")
     SCRATCH["xs%d" % _j] = ("sbuf", [128, 128], "uint8")
+    SEMAPHORES.append("arr%d" % _j)
+for _j in range(NP):
     SCRATCH["sgn%d" % _j] = ("sbuf", [128, NC], "bfloat16")
-    SEMAPHORES += ["arr%d" % _j, "mm%d" % _j, "sc%d" % _j, "ac%d" % _j]
-
-PRODUCTS = [(0, 0), (1, 0), (2, 0), (1, 1), (2, 1), (0, 1), (0, 2)]
+    SEMAPHORES += ["mm%d" % _j, "sc%d" % _j, "ac%d" % _j]
 
 
 def bits(m):
@@ -44,8 +52,52 @@ def bits(m):
 
 
 def rank_program(g, core, T, topo):
+    def peers(r, steps):
+        return [T.cores[RING[(RING.index(r) + k) % N]] for k in steps]
+
+    def relays(r):
+        me = T.cores[r]
+        return [c for c in range(GRID) if topo.chip(c) == topo.chip(me) and topo.die(c) != topo.die(me)
+                and T.rank_of(c) is None and all(topo.may_write(c, d) for d in peers(r, WTO[1:]))][:2]
+
+    def line(r):
+        m = topo.mask(T.cores[r], relays(r)[0])
+        for d in peers(r, XTO + WTO):
+            m &= topo.mask(T.cores[r], d)
+        return m
+
+    def beside(r):
+        return topo.mask(T.cores[r], relays(r)[0]) & ~line(r)
+
+    def send(transfers):
+        out = []
+        for view, mask, sem, to in transfers:
+            ids = []
+            for c, _ in to:
+                rid, pid, _ = topo.addr(c)
+                ids.append(DstId(rid=rid, pnc=pid))
+            out.append(RemoteDMATransfer(dst_ids=ids, dma_engine_mask=mask, remote_sem=sem, srcs=[view], dsts=[d for _, d in to]))
+        g.remote_dma_fused(out, local_sem=T.sem.sent)
+        return sum(bits(t[1]) for t in transfers)
+
+    def plane(w, cols):
+        return T["ws%d" % w][:, cols[0]:cols[1]]
+
+    def words(w, cols):
+        return T["wc%d" % w][:, cols[0]:cols[1]].bitcast(dt.uint8)
+
     rank = T.rank_of(core)
     if rank is None:
+        for r in range(N):
+            if core in relays(r):
+                w = 2 + relays(r).index(core)
+                to = peers(r, WTO)[w - 1]
+                mask, sem = topo.mask(core, to), T.sem["w%db" % w]
+                g.wait_ge(T.sem.plane, bits(beside(r)))
+                sent = send([(plane(0, HB), mask, sem, [(to, plane(w, HB))])])
+                g.wait_ge(T.sem.codes, bits(beside(r)))
+                sent += send([(words(0, HB), mask, sem, [(to, words(w, HB))])])
+                g.wait_ge(T.sem.sent, sent)
         return
     A = AluOpType
     place = RING.index(rank)
@@ -53,110 +105,111 @@ def rank_program(g, core, T, topo):
     def at(k):
         return RING[(place + k) % N]
 
-    def dst(r):
-        rid, pid, _ = topo.addr(T.cores[r])
-        return DstId(rid=rid, pnc=pid)
+    def in_count(c):
+        return bits(topo.mask(c, core))
 
-    def out_mask(r):
-        return topo.mask(core, T.cores[r])
+    def spot(p):
+        x, _, (lo, hi) = PRODUCTS[p]
+        n, j = len(PAIRS[x]), PAIRS[x].index(p)
+        last = 2 * n * (NC - 1) + 2 * j
+        return T["visit%d" % x], slice(last - 2 * n * (hi - lo - 1), last + 1, 2 * n), last
 
-    def in_count(r):
-        return bits(topo.mask(T.cores[r], core))
-
-    def spot(x, w):
-        buf, n = (T.home, HOME) if x == 0 else (T["visit%d" % x], VISIT)
-        last = 2 * n * (NC - 1) + 2 * w
-        return buf, slice(2 * w, last + 1, 2 * n), last
+    def logits(p):
+        _, _, (lo, hi) = PRODUCTS[p]
+        first = 512 * (p % BANKS)
+        return T.acc[:, first:first + hi - lo]
 
     xrank = [rank] + [at(-k) for k in XTO]
-    shards = [at(-k) for k in (0,) + WTO] + [at(k - v) for k in XTO for v in (0, WTO[0])]
+    wrank = [rank] + [at(-k) for k in WTO]
+    columns = [NC * at(k - (0,) [0] - ((0,) + WTO)[PRODUCTS[p][1]]) + PRODUCTS[p][2][0]
+               for x, k in enumerate((0,) + XTO) for p in PAIRS[x]]
 
     g.sync.dma_start(T.xb[:], T.x[:]).then_inc(T.sem.ldx, 16)
     g.sync.dma_start(T.wb[:], T.w[:]).then_inc(T.sem.ldw, 16)
 
-    sent = 0
-    xc, xs = T["xc%d" % rank], T["xs%d" % rank]
-    dests = [at(k) for k in XTO]
-    xmask = out_mask(dests[0])
-    for r in dests:
-        xmask &= out_mask(r)
+    xc, xs, arr = T["xc%d" % rank], T["xs%d" % rank], T.sem["arr%d" % rank]
+    xwords = xc[:].bitcast(dt.uint8)
+    x1, x2, w1, w2, _ = peers(rank, XTO + WTO)
+    out, near = line(rank), beside(rank)
     g.wait_ge(T.sem.qx, 1)
-    for view in (xs[:], xc[:].bitcast(dt.uint8)):
-        g.remote_dma_fused([RemoteDMATransfer(dst_ids=[dst(r) for r in dests], dma_engine_mask=xmask,
-                                              remote_sem=T.sem["arr%d" % rank], srcs=[view], dsts=[view for _ in dests])],
-                           local_sem=T.sem.sent)
-        sent += bits(xmask)
+    sent = send([(xs[:], out, arr, [(x1, xs[:]), (x2, xs[:])])])
+    sent += send([(xwords, out, arr, [(x1, xwords), (x2, xwords)])])
     g.wait_ge(T.sem.qw, 1)
-    for w, k in enumerate(WTO, 1):
-        r = at(k)
-        rid, pid, _ = topo.addr(T.cores[r])
-        for out, view in ((T["ws%d" % w][:], T.ws0[:]), (T["wc%d" % w][:].bitcast(dt.uint8), T.wc0[:].bitcast(dt.uint8))):
-            g.remote_dma(out, view, T.sem["warr%d" % w], T.sem.sent, pid, rid, out_mask(r))
-            sent += bits(out_mask(r))
-    for x in range(1, 1 + len(XTO)):
-        r = xrank[x]
-        rid, pid, _ = topo.addr(T.cores[r])
-        for p, (px, _) in enumerate(PRODUCTS):
-            if px == x:
-                g.wait_ge(T.sem["ac%d" % p], 1)
-        buf, _, first = spot(x, 0)
-        land = LAND + 2 * VISIT * (x - 1)
-        g.remote_dma(T.home[:, land:land + 2 * VISIT], buf[:, first:first + 2 * VISIT], T.sem.back, T.sem.sent, pid, rid, out_mask(r))
-        sent += bits(out_mask(r))
+    sent += send([(plane(0, HB), near, T.sem.plane, [(c, plane(0, HB)) for c in relays(rank)])])
+    sent += send([(plane(0, ALL), out, T.sem.w1a, [(w1, plane(1, ALL))])])
+    sent += send([(words(0, HB), near, T.sem.codes, [(c, words(0, HB)) for c in relays(rank)]),
+                  (words(0, HA), out, T.sem.w1a, [(w1, words(1, HA))])])
+    sent += send([(words(0, HB), out, T.sem.w1b, [(w1, words(1, HB))])])
+    sent += send([(plane(0, HA), out, T.sem.w2a, [(w2, plane(2, HA))])])
+    sent += send([(words(0, HA), out, T.sem.w2a, [(w2, words(2, HA))])])
+    for x in sorted((1, 2), key=lambda v: PAIRS[v][-1]):
+        to = T.cores[xrank[x]]
+        for p in PAIRS[x]:
+            g.wait_ge(T.sem["ac%d" % p], 1)
+        n = 2 * len(PAIRS[x])
+        buf, _, first = spot(PAIRS[x][0])
+        land = LAND + sum(2 * len(PAIRS[v]) for v in range(1, x))
+        sent += send([(buf[:, first:first + n], topo.mask(core, to), T.sem.back, [(to, T.visit0[:, land:land + n])])])
     g.wait_ge(T.sem.sent, sent)
 
-    g.vector.memset(T.low[:], LOW).then_inc(T.sem.low, 1)
-    for i, r in enumerate(shards):
-        g.vector.memset(T.off[:, i:i + 1], float(NC * r)).then_inc(T.sem.off, 1)
-    g.vector.memset(T.step1[:], BIG).then_inc(T.sem.large, 1)
     g.vector.wait_ge(T.sem.ldx, 16)
     g.vector.quantize_mx(xc[:], xs[:], T.xb[:]).then_inc(T.sem.qx, 1)
     g.vector.wait_ge(T.sem.ldw, 16)
     g.vector.quantize_mx(T.wc0[:], T.ws0[:], T.wb[:]).then_inc(T.sem.qw, 1)
+    g.vector.memset(T.low[:], LOW).then_inc(T.sem.low, 1)
+    for i, (c, after) in enumerate(zip(columns, columns[1:] + [0])):
+        g.vector.memset(T.step0[:, 3 * i + 2:3 * i + 3], float(c - after)).then_inc(T.sem.turn, 1)
+    g.vector.memset(T.step1[:], BIG).then_inc(T.sem.large, 1)
     g.vector.wait_ge(T.sem.low, 1)
-    for p, (x, w) in enumerate(PRODUCTS):
-        buf, cols, _ = spot(x, w)
+    for p, (_, _, (lo, hi)) in enumerate(PRODUCTS):
+        buf, cols, _ = spot(p)
         g.vector.wait_ge(T.sem["mm%d" % p], 1)
-        g.vector.tensor_tensor_scan(buf[:, cols], T.acc[:, 512 * p:512 * p + NC], T.low[:], LOW,
-                                    A.max, A.max).then_inc(T.sem["sc%d" % p], 1)
+        g.vector.tensor_tensor_scan(buf[:, cols], logits(p), T.low[:, 0:hi - lo], LOW, A.max, A.max).then_inc(T.sem["sc%d" % p], 1)
 
+    from1, from2 = xrank[1:]
+    landed = {("x", 1): (T.sem["arr%d" % from1], [T.cores[from1]] * 2),
+              ("x", 2): (T.sem["arr%d" % from2], [T.cores[from2]] * 2),
+              (1, 0): (T.sem.w1a, [T.cores[wrank[1]]] * 2),
+              (1, NH): (T.sem.w1b, [T.cores[wrank[1]]]),
+              (2, 0): (T.sem.w2a, [T.cores[wrank[2]]] * 2),
+              (2, NH): (T.sem.w2b, [relays(wrank[2])[0]] * 2),
+              (3, NH): (T.sem.w3b, [relays(wrank[3])[1]] * 2)}
     g.tensor.wait_ge(T.sem.qx, 1)
     g.tensor.wait_ge(T.sem.qw, 1)
-    seen = {("x", 0), ("w", 0)}
-    for p, (x, w) in enumerate(PRODUCTS):
-        if ("x", x) not in seen:
-            seen.add(("x", x))
-            g.tensor.wait_ge(T.sem["arr%d" % xrank[x]], 2 * in_count(xrank[x]))
-        if ("w", w) not in seen:
-            seen.add(("w", w))
-            g.tensor.wait_ge(T.sem["warr%d" % w], 2 * in_count(at(-WTO[w - 1])))
-        g.tensor.matmul_mx(T.acc[:, 512 * p:512 * p + NC], T["xc%d" % xrank[x]][:], T["xs%d" % xrank[x]][:],
-                           T["wc%d" % w][:], T["ws%d" % w][:], True, True).then_inc(T.sem["mm%d" % p], 1)
+    for p, (x, w, (lo, hi)) in enumerate(PRODUCTS):
+        for key in [("x", x)] + [(w, c) for c in range(lo, hi, NH)]:
+            if key in landed:
+                sem, senders = landed.pop(key)
+                g.tensor.wait_ge(sem, sum(in_count(c) for c in senders))
+        if p >= BANKS:
+            g.tensor.wait_ge(T.sem["sc%d" % (p - BANKS)], 1)
+        g.tensor.matmul_mx(logits(p), T["xc%d" % xrank[x]][:], T["xs%d" % xrank[x]][:],
+                           T["wc%d" % w][:, lo:hi], plane(w, (lo, hi)), True, True).then_inc(T.sem["mm%d" % p], 1)
 
-    for p, (x, w) in enumerate(PRODUCTS):
-        buf, cols, last = spot(x, w)
+    for p, (_, _, (lo, hi)) in enumerate(PRODUCTS):
+        buf, cols, last = spot(p)
         g.scalar.wait_ge(T.sem["sc%d" % p], 1)
-        g.scalar.activation(T["sgn%d" % p][:], buf[:, cols], ActivationFunctionType.Sign, bias=buf[:, last:last + 1],
+        g.scalar.activation(T["sgn%d" % p][:, 0:hi - lo], buf[:, cols], ActivationFunctionType.Sign, bias=buf[:, last:last + 1],
                             scale=-1.0, accum_out=buf[:, last + 1:last + 2]).then_inc(T.sem["ac%d" % p], 1)
 
-    end = FIRST + 2 * N
-    maxima, indices = T.home[:, FIRST:end:2], T.home[:, FIRST + 1:end:2]
-    best = T.res[:, 4 * N - 2:4 * N - 1]
-    g.vector.wait_ge(T.sem.off, N)
-    g.vector.wait_ge(T.sem.large, 1)
-    for p, (x, w) in enumerate(PRODUCTS):
-        if x == 0:
-            g.vector.wait_ge(T.sem["ac%d" % p], 1)
-    g.vector.wait_ge(T.sem.back, sum(in_count(r) for r in dests))
+    end = FIRST + 2 * NP
+    maxima, indices = T.visit0[:, FIRST:end:2], T.visit0[:, FIRST + 1:end:2]
+    best = T.res[:, 2 * STEPS - 2:2 * STEPS - 1]
+    for queue in (g.scalar, g.vector):
+        for p in PAIRS[0]:
+            queue.wait_ge(T.sem["ac%d" % p], 1)
+        queue.wait_ge(T.sem.large, 1)
+        queue.wait_ge(T.sem.back, sum(in_count(c) for c in peers(rank, XTO)))
+    g.scalar.activation(T.step1[:, 0:STEPS:3], indices, ActivationFunctionType.Copy).then_inc(T.sem.m2, 1)
     g.vector.tensor_reduce(best, maxima, AxisListType.X, A.max).then_inc(T.sem.m1, 1)
-    g.vector.tensor_tensor(T.step1[:, 0:2 * N:2], indices, T.off[:], A.add).then_inc(T.sem.m2, 1)
     g.vector.wait_ge(T.sem.m1, 1)
-    g.vector.tensor_scalar(T.step0[:, 0:2 * N:2], maxima, best, -BIG, A.is_lt, A.mult).then_inc(T.sem.m3, 1)
-    g.vector.tensor_scalar(T.step0[:, 1:2 * N:2], maxima, best, BIG, A.is_lt, A.mult).then_inc(T.sem.m3, 1)
+    g.vector.tensor_scalar(T.step0[:, 0:STEPS:3], maxima, best, -BIG, A.is_lt, A.mult).then_inc(T.sem.m3, 1)
+    g.vector.tensor_scalar(T.step0[:, 1:STEPS:3], maxima, best, BIG, A.is_lt, A.mult).then_inc(T.sem.m3, 1)
+    g.vector.wait_ge(T.sem.turn, NP)
     g.vector.wait_ge(T.sem.m2, 1)
     g.vector.wait_ge(T.sem.m3, 2)
-    g.vector.tensor_tensor_scan(T.res[:, 1:4 * N:2], T.step0[:], T.step1[:], BIG, A.add, A.min).then_inc(T.sem.m4, 1)
+    g.vector.tensor_tensor_scan(T.res[:, 1:2 * STEPS:2], T.step0[:], T.step1[:], BIG, A.add, A.min).then_inc(T.sem.m4, 1)
 
     g.sync.wait_ge(T.sem.m4, 1)
-    g.sync.dma_start(T.y[:], T.res[:, 4 * N - 2:4 * N]).then_inc(T.sem.stored, 16)
+    g.sync.dma_start(T.y[:], T.res[:, 2 * STEPS - 2:2 * STEPS]).then_inc(T.sem.stored, 16)
     g.sync.wait_ge(T.sem.stored, 16)

from concourse.bass import DstId, RemoteDMATransfer
from concourse.mybir import dt, AluOpType, AxisListType, ActivationFunctionType

N = 7
GRID = 128
NC = 256
NH = NC // 2
LOW = -9.0e29
BIG = 65536.0

RING = (0, 2, 1, 5, 3, 6, 4)
XTO = (5, 3)
WTO = (1, 6, 5)

ALL, HA, HB = (0, NC), (0, NH), (NH, NC)
PRODUCTS = [(0, 0, ALL), (1, 0, ALL), (2, 0, ALL), (2, 1, HA), (1, 1, HA), (1, 1, HB), (0, 1, ALL), (0, 2, HB), (0, 2, HA), (0, 3, HB)]
PAIRS = [[p for p in range(len(PRODUCTS)) if PRODUCTS[p][0] == x] for x in range(3)]
NP = len(PRODUCTS)
BANKS = 8
LAND = 2 * len(PAIRS[0]) * NC
FIRST = LAND - 2 * len(PAIRS[0])
STEPS = 3 * NP

SCRATCH = {
    "xb": ("sbuf", [128, 512], "bfloat16"),
    "wb": ("sbuf", [128, 4 * NC], "bfloat16"),
    "low": ("sbuf", [128, NC], "float32"),
    "step0": ("sbuf", [128, STEPS], "float32"),
    "step1": ("sbuf", [128, STEPS], "float32"),
    "res": ("sbuf", [128, 2 * STEPS], "float32"),
    "visit0": ("sbuf", [128, LAND + 2 * (len(PAIRS[1]) + len(PAIRS[2]))], "float32"),
    "visit1": ("sbuf", [128, 2 * len(PAIRS[1]) * NC], "float32"),
    "visit2": ("sbuf", [128, 2 * len(PAIRS[2]) * NC], "float32"),
    "acc": ("psum", [128, 512 * BANKS], "float32"),
}
SEMAPHORES = ["ldx", "ldw", "low", "turn", "large", "qx", "qw", "w1a", "w1b", "w2a", "w2b", "w3b", "plane", "codes",
              "sent", "back", "m1", "m2", "m3", "m4", "stored"]
for _j in range(4):
    SCRATCH["wc%d" % _j] = ("sbuf", [128, NC], "float8_e4m3fn_x4")
    SCRATCH["ws%d" % _j] = ("sbuf", [128, NC], "uint8")
for _j in range(N):
    SCRATCH["xc%d" % _j] = ("sbuf", [128, 128], "float8_e4m3fn_x4")
    SCRATCH["xs%d" % _j] = ("sbuf", [128, 128], "uint8")
    SEMAPHORES.append("arr%d" % _j)
for _j in range(NP):
    SCRATCH["sgn%d" % _j] = ("sbuf", [128, NC], "bfloat16")
    SEMAPHORES += ["mm%d" % _j, "sc%d" % _j, "ac%d" % _j]


def bits(m):
    return bin(m).count("1")


def rank_program(g, core, T, topo):
    def peers(r, steps):
        return [T.cores[RING[(RING.index(r) + k) % N]] for k in steps]

    def relays(r):
        me = T.cores[r]
        return [c for c in range(GRID) if topo.chip(c) == topo.chip(me) and topo.die(c) != topo.die(me)
                and T.rank_of(c) is None and all(topo.may_write(c, d) for d in peers(r, WTO[1:]))][:2]

    def line(r):
        m = topo.mask(T.cores[r], relays(r)[0])
        for d in peers(r, XTO + WTO):
            m &= topo.mask(T.cores[r], d)
        return m

    def beside(r):
        return topo.mask(T.cores[r], relays(r)[0]) & ~line(r)

    def send(transfers):
        out = []
        for view, mask, sem, to in transfers:
            ids = []
            for c, _ in to:
                rid, pid, _ = topo.addr(c)
                ids.append(DstId(rid=rid, pnc=pid))
            out.append(RemoteDMATransfer(dst_ids=ids, dma_engine_mask=mask, remote_sem=sem, srcs=[view], dsts=[d for _, d in to]))
        g.remote_dma_fused(out, local_sem=T.sem.sent)
        return sum(bits(t[1]) for t in transfers)

    def plane(w, cols):
        return T["ws%d" % w][:, cols[0]:cols[1]]

    def words(w, cols):
        return T["wc%d" % w][:, cols[0]:cols[1]].bitcast(dt.uint8)

    rank = T.rank_of(core)
    if rank is None:
        for r in range(N):
            if core in relays(r):
                w = 2 + relays(r).index(core)
                to = peers(r, WTO)[w - 1]
                mask, sem = topo.mask(core, to), T.sem["w%db" % w]
                g.wait_ge(T.sem.plane, bits(beside(r)))
                sent = send([(plane(0, HB), mask, sem, [(to, plane(w, HB))])])
                g.wait_ge(T.sem.codes, bits(beside(r)))
                sent += send([(words(0, HB), mask, sem, [(to, words(w, HB))])])
                g.wait_ge(T.sem.sent, sent)
        return
    A = AluOpType
    place = RING.index(rank)

    def at(k):
        return RING[(place + k) % N]

    def in_count(c):
        return bits(topo.mask(c, core))

    def spot(p):
        x, _, (lo, hi) = PRODUCTS[p]
        n, j = len(PAIRS[x]), PAIRS[x].index(p)
        last = 2 * n * (NC - 1) + 2 * j
        return T["visit%d" % x], slice(last - 2 * n * (hi - lo - 1), last + 1, 2 * n), last

    def logits(p):
        _, _, (lo, hi) = PRODUCTS[p]
        first = 512 * (p % BANKS)
        return T.acc[:, first:first + hi - lo]

    xrank = [rank] + [at(-k) for k in XTO]
    wrank = [rank] + [at(-k) for k in WTO]
    columns = [NC * at(k - (0,) [0] - ((0,) + WTO)[PRODUCTS[p][1]]) + PRODUCTS[p][2][0]
               for x, k in enumerate((0,) + XTO) for p in PAIRS[x]]

    g.sync.dma_start(T.xb[:], T.x[:]).then_inc(T.sem.ldx, 16)
    g.sync.dma_start(T.wb[:], T.w[:]).then_inc(T.sem.ldw, 16)

    xc, xs, arr = T["xc%d" % rank], T["xs%d" % rank], T.sem["arr%d" % rank]
    xwords = xc[:].bitcast(dt.uint8)
    x1, x2, w1, w2, _ = peers(rank, XTO + WTO)
    out, near = line(rank), beside(rank)
    g.wait_ge(T.sem.qx, 1)
    sent = send([(xs[:], out, arr, [(x1, xs[:]), (x2, xs[:])])])
    sent += send([(xwords, out, arr, [(x1, xwords), (x2, xwords)])])
    g.wait_ge(T.sem.qw, 1)
    sent += send([(plane(0, HB), near, T.sem.plane, [(c, plane(0, HB)) for c in relays(rank)])])
    sent += send([(plane(0, ALL), out, T.sem.w1a, [(w1, plane(1, ALL))])])
    sent += send([(words(0, HB), near, T.sem.codes, [(c, words(0, HB)) for c in relays(rank)]),
                  (words(0, HA), out, T.sem.w1a, [(w1, words(1, HA))])])
    sent += send([(words(0, HB), out, T.sem.w1b, [(w1, words(1, HB))])])
    sent += send([(plane(0, HA), out, T.sem.w2a, [(w2, plane(2, HA))])])
    sent += send([(words(0, HA), out, T.sem.w2a, [(w2, words(2, HA))])])
    for x in sorted((1, 2), key=lambda v: PAIRS[v][-1]):
        to = T.cores[xrank[x]]
        for p in PAIRS[x]:
            g.wait_ge(T.sem["ac%d" % p], 1)
        n = 2 * len(PAIRS[x])
        buf, _, first = spot(PAIRS[x][0])
        land = LAND + sum(2 * len(PAIRS[v]) for v in range(1, x))
        sent += send([(buf[:, first:first + n], topo.mask(core, to), T.sem.back, [(to, T.visit0[:, land:land + n])])])
    g.wait_ge(T.sem.sent, sent)

    g.vector.wait_ge(T.sem.ldx, 16)
    g.vector.quantize_mx(xc[:], xs[:], T.xb[:]).then_inc(T.sem.qx, 1)
    g.vector.wait_ge(T.sem.ldw, 16)
    g.vector.quantize_mx(T.wc0[:], T.ws0[:], T.wb[:]).then_inc(T.sem.qw, 1)
    g.vector.memset(T.low[:], LOW).then_inc(T.sem.low, 1)
    for i, (c, after) in enumerate(zip(columns, columns[1:] + [0])):
        g.vector.memset(T.step0[:, 3 * i + 2:3 * i + 3], float(c - after)).then_inc(T.sem.turn, 1)
    g.vector.memset(T.step1[:], BIG).then_inc(T.sem.large, 1)
    g.vector.wait_ge(T.sem.low, 1)
    for p, (_, _, (lo, hi)) in enumerate(PRODUCTS):
        buf, cols, _ = spot(p)
        g.vector.wait_ge(T.sem["mm%d" % p], 1)
        g.vector.tensor_tensor_scan(buf[:, cols], logits(p), T.low[:, 0:hi - lo], LOW, A.max, A.max).then_inc(T.sem["sc%d" % p], 1)

    from1, from2 = xrank[1:]
    landed = {("x", 1): (T.sem["arr%d" % from1], [T.cores[from1]] * 2),
              ("x", 2): (T.sem["arr%d" % from2], [T.cores[from2]] * 2),
              (1, 0): (T.sem.w1a, [T.cores[wrank[1]]] * 2),
              (1, NH): (T.sem.w1b, [T.cores[wrank[1]]]),
              (2, 0): (T.sem.w2a, [T.cores[wrank[2]]] * 2),
              (2, NH): (T.sem.w2b, [relays(wrank[2])[0]] * 2),
              (3, NH): (T.sem.w3b, [relays(wrank[3])[1]] * 2)}
    g.tensor.wait_ge(T.sem.qx, 1)
    g.tensor.wait_ge(T.sem.qw, 1)
    for p, (x, w, (lo, hi)) in enumerate(PRODUCTS):
        for key in [("x", x)] + [(w, c) for c in range(lo, hi, NH)]:
            if key in landed:
                sem, senders = landed.pop(key)
                g.tensor.wait_ge(sem, sum(in_count(c) for c in senders))
        if p >= BANKS:
            g.tensor.wait_ge(T.sem["sc%d" % (p - BANKS)], 1)
        g.tensor.matmul_mx(logits(p), T["xc%d" % xrank[x]][:], T["xs%d" % xrank[x]][:],
                           T["wc%d" % w][:, lo:hi], plane(w, (lo, hi)), True, True).then_inc(T.sem["mm%d" % p], 1)

    for p, (_, _, (lo, hi)) in enumerate(PRODUCTS):
        buf, cols, last = spot(p)
        g.scalar.wait_ge(T.sem["sc%d" % p], 1)
        g.scalar.activation(T["sgn%d" % p][:, 0:hi - lo], buf[:, cols], ActivationFunctionType.Sign, bias=buf[:, last:last + 1],
                            scale=-1.0, accum_out=buf[:, last + 1:last + 2]).then_inc(T.sem["ac%d" % p], 1)

    end = FIRST + 2 * NP
    maxima, indices = T.visit0[:, FIRST:end:2], T.visit0[:, FIRST + 1:end:2]
    best = T.res[:, 2 * STEPS - 2:2 * STEPS - 1]
    for queue in (g.scalar, g.vector):
        for p in PAIRS[0]:
            queue.wait_ge(T.sem["ac%d" % p], 1)
        queue.wait_ge(T.sem.large, 1)
        queue.wait_ge(T.sem.back, sum(in_count(c) for c in peers(rank, XTO)))
    g.scalar.activation(T.step1[:, 0:STEPS:3], indices, ActivationFunctionType.Copy).then_inc(T.sem.m2, 1)
    g.vector.tensor_reduce(best, maxima, AxisListType.X, A.max).then_inc(T.sem.m1, 1)
    g.vector.wait_ge(T.sem.m1, 1)
    g.vector.tensor_scalar(T.step0[:, 0:STEPS:3], maxima, best, -BIG, A.is_lt, A.mult).then_inc(T.sem.m3, 1)
    g.vector.tensor_scalar(T.step0[:, 1:STEPS:3], maxima, best, BIG, A.is_lt, A.mult).then_inc(T.sem.m3, 1)
    g.vector.wait_ge(T.sem.turn, NP)
    g.vector.wait_ge(T.sem.m2, 1)
    g.vector.wait_ge(T.sem.m3, 2)
    g.vector.tensor_tensor_scan(T.res[:, 1:2 * STEPS:2], T.step0[:], T.step1[:], BIG, A.add, A.min).then_inc(T.sem.m4, 1)

    g.sync.wait_ge(T.sem.m4, 1)
    g.sync.dma_start(T.y[:], T.res[:, 2 * STEPS - 2:2 * STEPS]).then_inc(T.sem.stored, 16)
    g.sync.wait_ge(T.sem.stored, 16)
